import numpy as np
import ml_dtypes


def mxq(x, axis, fmt="e4m3"):
    dtype, down = {"e4m3": (ml_dtypes.float8_e4m3fn, 7), "e5m2": (ml_dtypes.float8_e5m2, 14)}[fmt]
    v = np.moveaxis(np.asarray(x, np.float32).astype(ml_dtypes.bfloat16).astype(np.float64), axis, -1)
    blocks = v.reshape(v.shape[:-1] + (-1, 32))
    amax = np.abs(blocks).max(-1, keepdims=True)
    byte = np.maximum(np.where(amax > 0, np.frexp(amax)[1] - 1 + 127, 0) - down, 1)
    scale = np.exp2(byte - 127.0)
    codes = (blocks / scale).astype(np.float32).astype(dtype).astype(np.float64)
    return np.moveaxis((codes * scale).reshape(v.shape), -1, axis)


WIDE = False


def mx_kscale(k):
    if not WIDE:
        return np.ones(k)
    levels = np.array([10, -10, 5, -5, 0])
    if k % 512:
        return np.exp2(np.random.permutation(np.resize(levels, k // 32))).repeat(32)
    a = np.empty((k // 512, 16))
    for p in range(k // 512):
        a[p, :8] = np.random.permutation(np.resize(levels, 8))
        for g in range(8):
            far = levels[np.abs(levels - a[p, g]) >= 10]
            a[p, g + 8] = far[np.random.randint(len(far))]
    return np.exp2(a.ravel()).repeat(32)


def f64(x):
    return np.asarray(x).astype(np.float64)


def striped(idx):
    return np.tile(idx.reshape(-1, 16).T, (8, 1)).astype(np.uint16)


def unstriped(offs):
    return offs[:16].T.reshape(-1).astype(np.int64)


def pack_weight(w):
    k, n = w.shape
    w = f64(np.asarray(w, np.float32).astype(ml_dtypes.bfloat16)).reshape(k // 32, 32, n)
    amax = np.abs(w).max(1)
    byte = np.clip(np.where(amax > 0, np.frexp(amax)[1] - 1 + 127 - 7, 1), 1, 254)
    scaled = (w * np.exp2(127.0 - byte)[:, None, :]).reshape(k, n).astype(np.float32)
    words = np.ascontiguousarray(scaled.reshape(k // 512, 128, 4, n).transpose(0, 1, 3, 2)).astype(ml_dtypes.float8_e4m3fn).view(np.uint8)
    return words, np.ascontiguousarray(byte.astype(np.uint8).reshape(k // 512, 16, n))


def unpack_weight(words, scales):
    g, p, n, _ = words.shape
    vals = np.ascontiguousarray(words).view(ml_dtypes.float8_e4m3fn).astype(np.float64) * np.repeat(np.exp2(scales.astype(np.float64) - 127.0), 8, axis=1)[..., None]
    return vals.transpose(0, 1, 3, 2).reshape(g * 512, n)


K, T, S, D, N = 1024, 2048, 1024, 4, 128
P = 2 ** 7


def setup_inputs():
    n = np.random.standard_normal
    s = mx_kscale(K)[:, None]
    packed_xT = pack_weight(n((K, T)) * s)
    return {
        "x_words": packed_xT[0],
        "x_scales": packed_xT[1],
        "w1": (n((K, N)) / np.sqrt(K) / s).astype(np.float32),
        "wt": (np.tile(np.random.uniform(0.5, 1.5, S), (P, 1))).astype(np.float32),
        "offs": striped(np.random.permutation(T)[:S]),
    }


def reference(x_words, x_scales, w1, wt, offs):
    xq = unpack_weight(x_words, x_scales)[:, unstriped(offs)]
    y = mxq(f64(w1), 0, "e4m3").T @ xq
    mg = y.reshape(len(y), -1, D).mean(axis=2)
    mt = mg.reshape(len(mg), -1, D).mean(axis=2)
    d2 = (mg - np.repeat(mt, D, axis=1)) ** 2
    vt = d2.reshape(len(d2), -1, D).mean(axis=2) + 0.05
    d1 = (y - np.repeat(mg, D, axis=1)) ** 2
    vg = d1.reshape(len(d1), -1, D).mean(axis=2) + 0.1
    shr = np.repeat(vt, D, axis=1) / (np.repeat(vt, D, axis=1) + 0.25 * vg)
    post = np.repeat(mt, D, axis=1) + shr * (mg - np.repeat(mt, D, axis=1))
    return ((y - np.repeat(post, D, axis=1)) ** 2) * f64(wt)[:1] + np.repeat(shr, D, axis=1)

@@ -1,0 +1,228 @@
+import math
+from contextlib import ExitStack
+
+import concourse.mybir as mybir
+
+K, T, S, D, N = 1024, 2048, 1024, 4, 128
+FLOPS = 2 * K * S * N
+
+F32 = mybir.dt.float32
+BF16 = mybir.dt.bfloat16
+I32 = mybir.dt.int32
+U32 = mybir.dt.uint32
+U16 = mybir.dt.uint16
+U8 = mybir.dt.uint8
+FP8X4 = mybir.dt.float8_e4m3fn_x4
+ACT = mybir.ActivationFunctionType
+ALU = mybir.AluOpType
+AXIS = mybir.AxisListType
+
+P = 128
+PACK = 4
+PASSES = K // (P * PACK)
+QUADRANT = 32
+SCALE_ROWS = 4
+LIST_COLUMN = 16
+CHUNKS = [256, 256, 256, 256]
+SKEW = 0
+PIECE = 256
+FINAL = 256
+
+
+def over_members(ap, groups):
+    return ap.unsqueeze(2).to_broadcast([P, groups, D])
+
+
+def by_group(ap):
+    return ap.rearrange("p (g d) -> p g d", d=D)
+
+
+def tile_picked_yhbays_res_p_kernel(tc, x_words, x_scales, w1, wt, offs, out):
+    nc = tc.nc
+    with ExitStack() as ctx:
+        keep = ctx.enter_context(tc.tile_pool(name="keep", bufs=1))
+        psum = ctx.enter_context(tc.psum_pool(name="psum", bufs=1))
+
+        offsets = keep.tile([P, S // LIST_COLUMN], U16, name="offsets")
+        word_window = [keep.tile([P, T], U32, name="word_window%d" % a) for a in range(PASSES)]
+        byte_window = keep.tile([P, T], U8, name="byte_window")
+        w_raw = keep.tile([P, PASSES, PACK, N], F32, name="w_raw", tag="w_then_wt")
+
+        warm_in = keep.tile([P, 1], F32, name="warm_in")
+        warm_out = keep.tile([P, 1], F32, name="warm_out")
+        nc.gpsimd.memset(warm_in[:], 1.0)
+        nc.scalar.activation(warm_out[:], warm_in[:], ACT.Abs_reciprocal_sqrt)
+
+        def load_words(a):
+            nc.sync.dma_start(
+                out=word_window[a][:].bitcast(I32),
+                in_=x_words[a].rearrange("p n t -> p (n t)").bitcast(I32),
+            )
+
+        nc.vector.memset(byte_window[:].bitcast(I32), 0)
+        load_words(0)
+        nc.sync.dma_start(offsets[:], offs)
+        load_words(1)
+        nc.sync.dma_start(
+            out=w_raw[:].rearrange("p a j n -> p a (j n)"),
+            in_=w1.rearrange("(a p j) n -> p a (j n)", a=PASSES, j=PACK),
+        )
+        for q in range(P // QUADRANT):
+            nc.sync.dma_start(
+                out=byte_window[QUADRANT * q : QUADRANT * q + PASSES * SCALE_ROWS, :].bitcast(I32),
+                in_=x_scales[:, SCALE_ROWS * q : SCALE_ROWS * (q + 1), :].bitcast(I32),
+            )
+
+        words = [keep.tile([P, S], U32, name="words%d" % a, align_bytes=64) for a in range(PASSES)]
+        for a in range(PASSES):
+            nc.vector.tensor_copy(words[a][:], word_window[a][:].indirect(offsets[:]))
+
+        w_grouped = keep.tile([P, PASSES, N, PACK], BF16, name="w_grouped", align_bytes=64)
+        w_codes = keep.tile([P, PASSES, N], U32, name="w_codes", align_bytes=64)
+        w_scales = keep.tile([P, PASSES, N], U8, name="w_scales", align_bytes=64)
+        nc.scalar.activation(w_grouped[:], w_raw[:].rearrange("p a j n -> p a n j"), ACT.Copy)
+        nc.vector.quantize_mx(
+            out=w_codes[:].rearrange("p a n -> p (a n)").bitcast(FP8X4),
+            scales=w_scales[:].rearrange("p a n -> p (a n)"),
+            in_=w_grouped[:].rearrange("p a n j -> p (a n j)"),
+        )
+
+        weights = keep.tile([P, S], F32, name="weights", tag="w_then_wt")
+        nc.sync.dma_start(out=weights[:], in_=wt)
+
+        def chunk_steps(c, j0, n):
+            nv = n // D
+            nw = nv // D
+
+            def sb(name, shape):
+                return keep.tile([P] + shape, F32, name="%s%d" % (name, c))
+
+            y = psum.tile([P, n], F32, name="y%d" % c)
+            upper = sb("upper", [2, nv])
+            pair_sum = sb("pair_sum", [2, nv])
+            pair_diff = sb("pair_diff", [2, nv])
+            pair_sq = sb("pair_sq", [2, nv])
+            sum4 = sb("sum4", [nv])
+            cross = sb("cross", [nv])
+            cross_sq = sb("cross_sq", [nv])
+            within = sb("within", [nv])
+            within_all = sb("within_all", [nv])
+            sum16 = sb("sum16", [nw])
+            gap4 = sb("gap4", [nv])
+            gap_sq = sb("gap_sq", [nv])
+            between = sb("between", [nw])
+            den = sb("den", [nv])
+            root = sb("root", [nv])
+            inv = sb("inv", [nv])
+            shr = sb("shr", [nv])
+            scaled_gap4 = sb("scaled_gap4", [nv])
+            pull4 = sb("pull4", [nv])
+            post4 = sb("post4", [nv])
+            resid = sb("resid", [n])
+            resid_sq = sb("resid_sq", [n])
+            weighted = sb("weighted", [n])
+            result = sb("result", [n])
+            members = y[:].rearrange("p (v d) -> p d v", d=D)
+
+            def product():
+                for i0 in range(0, n, PIECE):
+                    m = min(PIECE, n - i0)
+                    scale_bytes = keep.tile([P, m], U8, name="scale_bytes%d_%d" % (c, i0), align_bytes=64)
+                    first = (j0 + i0) // LIST_COLUMN
+                    nc.vector.tensor_copy(
+                        scale_bytes[:], byte_window[:].indirect(offsets[:, first : first + m // LIST_COLUMN])
+                    )
+                    for a in range(PASSES):
+                        nc.tensor.matmul_mx(
+                            out=y[:, i0 : i0 + m],
+                            lhsT=w_codes[:, a, :].bitcast(FP8X4),
+                            lhsT_scale=w_scales[:, a, :],
+                            rhs=words[a][:, j0 + i0 : j0 + i0 + m].bitcast(FP8X4),
+                            rhs_scale=scale_bytes[SCALE_ROWS * a : P, :],
+                            start=(a == 0),
+                            stop=(a == PASSES - 1),
+                        )
+                nc.scalar.copy(upper[:], members[:, 2:4, :])
+
+            def pairs():
+                nc.vector.tensor_tensor(pair_sum[:], members[:, 0:2, :], upper[:], ALU.add)
+                nc.vector.tensor_tensor(pair_diff[:], members[:, 0:2, :], upper[:], ALU.subtract)
+                nc.scalar.activation(pair_sq[:], pair_diff[:], ACT.Square, scale=math.sqrt(1.0 / 32.0))
+
+            def district_sums():
+                nc.vector.tensor_tensor(sum4[:], pair_sum[:, 0, :], pair_sum[:, 1, :], ALU.add)
+                nc.vector.tensor_tensor(cross[:], pair_sum[:, 0, :], pair_sum[:, 1, :], ALU.subtract)
+                nc.scalar.activation(cross_sq[:], cross[:], ACT.Square, scale=0.125)
+
+            def state_sums():
+                nc.vector.tensor_reduce(sum16[:], by_group(sum4[:]), AXIS.X, ALU.add)
+
+            def gaps():
+                nc.vector.scalar_tensor_tensor(
+                    by_group(gap4[:]), over_members(sum16[:], nw), -0.25, by_group(sum4[:]), ALU.mult, ALU.add
+                )
+                nc.scalar.activation(gap_sq[:], gap4[:], ACT.Square, scale=0.125)
+                nc.vector.tensor_tensor(within[:], pair_sq[:, 0, :], pair_sq[:, 1, :], ALU.add)
+
+            def within_variance():
+                nc.vector.scalar_tensor_tensor(within_all[:], within[:], 0.075, cross_sq[:], ALU.add, ALU.add)
+
+            def between_variance():
+                nc.vector.tensor_reduce(between[:], by_group(gap_sq[:]), AXIS.X, ALU.add)
+
+            def denominator():
+                nc.vector.tensor_tensor(by_group(den[:]), by_group(within_all[:]), over_members(between[:], nw), ALU.add)
+                nc.scalar.activation(root[:], den[:], ACT.Abs_reciprocal_sqrt)
+                nc.scalar.activation(inv[:], root[:], ACT.Square)
+
+            def numerator():
+                nc.vector.scalar_tensor_tensor(
+                    by_group(scaled_gap4[:]), over_members(between[:], nw), 0.05, by_group(gap4[:]), ALU.add, ALU.mult
+                )
+
+            def pull():
+                nc.vector.tensor_tensor(pull4[:], scaled_gap4[:], inv[:], ALU.mult)
+
+            def posterior():
+                nc.vector.scalar_tensor_tensor(
+                    by_group(post4[:]), over_members(sum16[:], nw), 0.25, by_group(pull4[:]), ALU.mult, ALU.add
+                )
+                nc.vector.scalar_tensor_tensor(
+                    by_group(shr[:]), over_members(between[:], nw), 0.05, by_group(inv[:]), ALU.add, ALU.mult
+                )
+
+            parts = [(i0, min(FINAL, n - i0)) for i0 in range(0, n, FINAL)]
+
+            def residual():
+                for i0, m in parts:
+                    js, vs = slice(i0, i0 + m), slice(i0 // D, (i0 + m) // D)
+                    nc.vector.scalar_tensor_tensor(
+                        by_group(resid[:, js]), over_members(post4[:, vs], m // D), -0.25, by_group(y[:, js]),
+                        ALU.mult, ALU.add,
+                    )
+                    nc.scalar.activation(resid_sq[:, js], resid[:, js], ACT.Square)
+
+            def weigh():
+                for i0, m in parts:
+                    js = slice(i0, i0 + m)
+                    nc.vector.tensor_tensor(weighted[:, js], resid_sq[:, js], weights[:, j0 + i0 : j0 + i0 + m], ALU.mult)
+
+            def finish():
+                for i0, m in parts:
+                    js, vs = slice(i0, i0 + m), slice(i0 // D, (i0 + m) // D)
+                    nc.vector.tensor_tensor(
+                        by_group(result[:, js]), by_group(weighted[:, js]), over_members(shr[:, vs], m // D), ALU.add
+                    )
+                    nc.sync.dma_start(out=out[:, j0 + i0 : j0 + i0 + m], in_=result[:, js])
+
+            return [product, pairs, district_sums, state_sums, gaps, within_variance, between_variance,
+                    denominator, numerator, pull, posterior, residual, weigh, finish]
+
+        starts = [sum(CHUNKS[:c]) for c in range(len(CHUNKS))]
+        steps = [chunk_steps(c, starts[c], CHUNKS[c]) for c in range(len(CHUNKS))]
+        depth = len(steps[0])
+        for tick in range(depth + SKEW * (len(CHUNKS) - 1)):
+            for c in range(len(CHUNKS)):
+                k = tick - SKEW * c
+                if 0 <= k < depth:
+                    steps[c][k]()

@@ -24,7 +24,7 @@ QUADRANT = 32
 SCALE_ROWS = 4
 LIST_COLUMN = 16
 CHUNKS = [256, 256, 256, 256]
-SKEW = 0
+SKEW = 1
 PIECE = 256
 FINAL = 256
 
@@ -48,34 +48,44 @@ def tile_picked_yhbays_res_p_kernel(tc, x_words, x_scales, w1, wt, offs, out):
         byte_window = keep.tile([P, T], U8, name="byte_window")
         w_raw = keep.tile([P, PASSES, PACK, N], F32, name="w_raw", tag="w_then_wt")
 
-        warm_in = keep.tile([P, 1], F32, name="warm_in")
-        warm_out = keep.tile([P, 1], F32, name="warm_out")
-        nc.gpsimd.memset(warm_in[:], 1.0)
-        nc.scalar.activation(warm_out[:], warm_in[:], ACT.Abs_reciprocal_sqrt)
-
         def load_words(a):
             nc.sync.dma_start(
                 out=word_window[a][:].bitcast(I32),
                 in_=x_words[a].rearrange("p n t -> p (n t)").bitcast(I32),
             )
 
-        nc.vector.memset(byte_window[:].bitcast(I32), 0)
-        load_words(0)
+        rows = PASSES * SCALE_ROWS
+        picked_bytes = keep.tile([P, S], U8, name="picked_bytes")
+        planes = keep.tile([P, S], U8, name="planes", align_bytes=64)
+        nc.vector.memset(byte_window[QUADRANT : 2 * QUADRANT, :].bitcast(I32), 0)
+        nc.vector.memset(byte_window[2 * QUADRANT : P, :].bitcast(I32), 0)
+        nc.vector.memset(planes[:].bitcast(I32), 0)
+        by_row = x_scales.rearrange("a (q r) n -> r q a n", r=SCALE_ROWS)
         nc.sync.dma_start(offsets[:], offs)
-        load_words(1)
+        for r in range(SCALE_ROWS):
+            queue = nc.sync if r < 2 else nc.scalar
+            queue.dma_start(out=byte_window[r:QUADRANT:SCALE_ROWS, :].bitcast(I32), in_=by_row[r].bitcast(I32))
+
+        warm_in = keep.tile([P, 1], F32, name="warm_in")
+        warm_out = keep.tile([P, 1], F32, name="warm_out")
+        nc.gpsimd.memset(warm_in[:], 1.0)
+        nc.scalar.activation(warm_out[:], warm_in[:], ACT.Abs_reciprocal_sqrt)
+
+        load_words(0)
         nc.sync.dma_start(
             out=w_raw[:].rearrange("p a j n -> p a (j n)"),
             in_=w1.rearrange("(a p j) n -> p a (j n)", a=PASSES, j=PACK),
         )
-        for q in range(P // QUADRANT):
-            nc.sync.dma_start(
-                out=byte_window[QUADRANT * q : QUADRANT * q + PASSES * SCALE_ROWS, :].bitcast(I32),
-                in_=x_scales[:, SCALE_ROWS * q : SCALE_ROWS * (q + 1), :].bitcast(I32),
-            )
+        load_words(1)
 
-        words = [keep.tile([P, S], U32, name="words%d" % a, align_bytes=64) for a in range(PASSES)]
-        for a in range(PASSES):
-            nc.vector.tensor_copy(words[a][:], word_window[a][:].indirect(offsets[:]))
+        nc.vector.tensor_copy(picked_bytes[:], byte_window[:].indirect(offsets[:]))
+        for q in range(P // QUADRANT):
+            nc.scalar.dma_start(
+                out=planes[QUADRANT * q : QUADRANT * q + rows, :].bitcast(I32),
+                in_=picked_bytes[rows * q : rows * (q + 1), :].bitcast(I32),
+            )
+        words0 = keep.tile([P, S], U32, name="words0", align_bytes=64)
+        nc.vector.tensor_copy(words0[:], word_window[0][:].indirect(offsets[:]))
 
         w_grouped = keep.tile([P, PASSES, N, PACK], BF16, name="w_grouped", align_bytes=64)
         w_codes = keep.tile([P, PASSES, N], U32, name="w_codes", align_bytes=64)
@@ -125,23 +135,21 @@ def tile_picked_yhbays_res_p_kernel(tc, x_words, x_scales, w1, wt, offs, out):
             members = y[:].rearrange("p (v d) -> p d v", d=D)
 
             def product():
-                for i0 in range(0, n, PIECE):
-                    m = min(PIECE, n - i0)
-                    scale_bytes = keep.tile([P, m], U8, name="scale_bytes%d_%d" % (c, i0), align_bytes=64)
-                    first = (j0 + i0) // LIST_COLUMN
-                    nc.vector.tensor_copy(
-                        scale_bytes[:], byte_window[:].indirect(offsets[:, first : first + m // LIST_COLUMN])
+                words1 = keep.tile([P, n], U32, name="words1_%d" % c, align_bytes=64)
+                first = j0 // LIST_COLUMN
+                nc.vector.tensor_copy(
+                    words1[:], word_window[1][:].indirect(offsets[:, first : first + n // LIST_COLUMN])
+                )
+                for a, moving in enumerate((words0[:, j0 : j0 + n], words1[:])):
+                    nc.tensor.matmul_mx(
+                        out=y[:],
+                        lhsT=w_codes[:, a, :].bitcast(FP8X4),
+                        lhsT_scale=w_scales[:, a, :],
+                        rhs=moving.bitcast(FP8X4),
+                        rhs_scale=planes[SCALE_ROWS * a : P, j0 : j0 + n],
+                        start=(a == 0),
+                        stop=(a == PASSES - 1),
                     )
-                    for a in range(PASSES):
-                        nc.tensor.matmul_mx(
-                            out=y[:, i0 : i0 + m],
-                            lhsT=w_codes[:, a, :].bitcast(FP8X4),
-                            lhsT_scale=w_scales[:, a, :],
-                            rhs=words[a][:, j0 + i0 : j0 + i0 + m].bitcast(FP8X4),
-                            rhs_scale=scale_bytes[SCALE_ROWS * a : P, :],
-                            start=(a == 0),
-                            stop=(a == PASSES - 1),
-                        )
                 nc.scalar.copy(upper[:], members[:, 2:4, :])
 
             def pairs():
@@ -191,7 +199,8 @@ def tile_picked_yhbays_res_p_kernel(tc, x_words, x_scales, w1, wt, offs, out):
                     by_group(shr[:]), over_members(between[:], nw), 0.05, by_group(inv[:]), ALU.add, ALU.mult
                 )
 
-            parts = [(i0, min(FINAL, n - i0)) for i0 in range(0, n, FINAL)]
+            width = 128 if c == len(CHUNKS) - 1 else FINAL
+            parts = [(i0, min(width, n - i0)) for i0 in range(0, n, width)]
 
             def residual():
                 for i0, m in parts:

@@ -54,17 +54,15 @@ def tile_picked_yhbays_res_p_kernel(tc, x_words, x_scales, w1, wt, offs, out):
                 in_=x_words[a].rearrange("p n t -> p (n t)").bitcast(I32),
             )
 
-        rows = PASSES * SCALE_ROWS
         picked_bytes = keep.tile([P, S], U8, name="picked_bytes")
         planes = keep.tile([P, S], U8, name="planes", align_bytes=64)
         nc.vector.memset(byte_window[QUADRANT : 2 * QUADRANT, :].bitcast(I32), 0)
         nc.vector.memset(byte_window[2 * QUADRANT : P, :].bitcast(I32), 0)
-        nc.vector.memset(planes[:].bitcast(I32), 0)
-        by_row = x_scales.rearrange("a (q r) n -> r q a n", r=SCALE_ROWS)
+        nc.sync.dma_start(
+            out=byte_window[0:QUADRANT, :].bitcast(I32),
+            in_=x_scales.rearrange("a q n -> (a q) n").bitcast(I32),
+        )
         nc.sync.dma_start(offsets[:], offs)
-        for r in range(SCALE_ROWS):
-            queue = nc.sync if r < 2 else nc.scalar
-            queue.dma_start(out=byte_window[r:QUADRANT:SCALE_ROWS, :].bitcast(I32), in_=by_row[r].bitcast(I32))
 
         warm_in = keep.tile([P, 1], F32, name="warm_in")
         warm_out = keep.tile([P, 1], F32, name="warm_out")
@@ -79,10 +77,17 @@ def tile_picked_yhbays_res_p_kernel(tc, x_words, x_scales, w1, wt, offs, out):
         load_words(1)
 
         nc.vector.tensor_copy(picked_bytes[:], byte_window[:].indirect(offsets[:]))
-        for q in range(P // QUADRANT):
-            nc.scalar.dma_start(
-                out=planes[QUADRANT * q : QUADRANT * q + rows, :].bitcast(I32),
-                in_=picked_bytes[rows * q : rows * (q + 1), :].bitcast(I32),
+        nc.vector.tensor_copy(planes[:].bitcast(I32), picked_bytes[:].bitcast(I32))
+        moves = [
+            (SCALE_ROWS * (a * (P // QUADRANT) + q), QUADRANT * q + SCALE_ROWS * a)
+            for a in range(PASSES)
+            for q in range(P // QUADRANT)
+        ]
+        for i, (source, target) in enumerate(moves[1:]):
+            queue = nc.scalar if i < 3 else nc.sync
+            queue.dma_start(
+                out=planes[target : target + SCALE_ROWS, :].bitcast(I32),
+                in_=picked_bytes[source : source + SCALE_ROWS, :].bitcast(I32),
             )
         words0 = keep.tile([P, S], U32, name="words0", align_bytes=64)
         nc.vector.tensor_copy(words0[:], word_window[0][:].indirect(offsets[:]))
@@ -140,16 +145,18 @@ def tile_picked_yhbays_res_p_kernel(tc, x_words, x_scales, w1, wt, offs, out):
                 nc.vector.tensor_copy(
                     words1[:], word_window[1][:].indirect(offsets[:, first : first + n // LIST_COLUMN])
                 )
-                for a, moving in enumerate((words0[:, j0 : j0 + n], words1[:])):
-                    nc.tensor.matmul_mx(
-                        out=y[:],
-                        lhsT=w_codes[:, a, :].bitcast(FP8X4),
-                        lhsT_scale=w_scales[:, a, :],
-                        rhs=moving.bitcast(FP8X4),
-                        rhs_scale=planes[SCALE_ROWS * a : P, j0 : j0 + n],
-                        start=(a == 0),
-                        stop=(a == PASSES - 1),
-                    )
+                for i0 in range(0, n, PIECE):
+                    m = min(PIECE, n - i0)
+                    for a, moving in enumerate((words0[:, j0 + i0 : j0 + i0 + m], words1[:, i0 : i0 + m])):
+                        nc.tensor.matmul_mx(
+                            out=y[:, i0 : i0 + m],
+                            lhsT=w_codes[:, a, :].bitcast(FP8X4),
+                            lhsT_scale=w_scales[:, a, :],
+                            rhs=moving.bitcast(FP8X4),
+                            rhs_scale=planes[SCALE_ROWS * a : P, j0 + i0 : j0 + i0 + m],
+                            start=(a == 0),
+                            stop=(a == PASSES - 1),
+                        )
                 nc.scalar.copy(upper[:], members[:, 2:4, :])
 
             def pairs():

import math
from contextlib import ExitStack

import concourse.mybir as mybir

K, T, S, D, N = 1024, 2048, 1024, 4, 128
FLOPS = 2 * K * S * N

F32 = mybir.dt.float32
BF16 = mybir.dt.bfloat16
I32 = mybir.dt.int32
U32 = mybir.dt.uint32
U16 = mybir.dt.uint16
U8 = mybir.dt.uint8
FP8X4 = mybir.dt.float8_e4m3fn_x4
ACT = mybir.ActivationFunctionType
ALU = mybir.AluOpType
AXIS = mybir.AxisListType

P = 128
PACK = 4
PASSES = K // (P * PACK)
QUADRANT = 32
SCALE_ROWS = 4
LIST_COLUMN = 16
CHUNKS = [256, 256, 256, 256]
SKEW = 1
PIECE = 256
FINAL = 256


def over_members(ap, groups):
    return ap.unsqueeze(2).to_broadcast([P, groups, D])


def by_group(ap):
    return ap.rearrange("p (g d) -> p g d", d=D)


def tile_picked_yhbays_res_p_kernel(tc, x_words, x_scales, w1, wt, offs, out):
    nc = tc.nc
    with ExitStack() as ctx:
        keep = ctx.enter_context(tc.tile_pool(name="keep", bufs=1))
        psum = ctx.enter_context(tc.psum_pool(name="psum", bufs=1))

        offsets = keep.tile([P, S // LIST_COLUMN], U16, name="offsets")
        word_window = [keep.tile([P, T], U32, name="word_window%d" % a) for a in range(PASSES)]
        byte_window = keep.tile([P, T], U8, name="byte_window")
        w_raw = keep.tile([P, PASSES, PACK, N], F32, name="w_raw", tag="w_then_wt")

        def load_words(a):
            nc.sync.dma_start(
                out=word_window[a][:].bitcast(I32),
                in_=x_words[a].rearrange("p n t -> p (n t)").bitcast(I32),
            )

        picked_bytes = keep.tile([P, S], U8, name="picked_bytes")
        planes = keep.tile([P, S], U8, name="planes", align_bytes=64)
        nc.vector.memset(byte_window[QUADRANT : 2 * QUADRANT, :].bitcast(I32), 0)
        nc.vector.memset(byte_window[2 * QUADRANT : P, :].bitcast(I32), 0)
        nc.sync.dma_start(
            out=byte_window[0:QUADRANT, :].bitcast(I32),
            in_=x_scales.rearrange("a q n -> (a q) n").bitcast(I32),
        )
        nc.sync.dma_start(offsets[:], offs)

        warm_in = keep.tile([P, 1], F32, name="warm_in")
        warm_out = keep.tile([P, 1], F32, name="warm_out")
        nc.gpsimd.memset(warm_in[:], 1.0)
        nc.scalar.activation(warm_out[:], warm_in[:], ACT.Abs_reciprocal_sqrt)

        load_words(0)
        nc.sync.dma_start(
            out=w_raw[:].rearrange("p a j n -> p a (j n)"),
            in_=w1.rearrange("(a p j) n -> p a (j n)", a=PASSES, j=PACK),
        )
        load_words(1)

        nc.vector.tensor_copy(picked_bytes[:], byte_window[:].indirect(offsets[:]))
        nc.vector.tensor_copy(planes[:].bitcast(I32), picked_bytes[:].bitcast(I32))
        moves = [
            (SCALE_ROWS * (a * (P // QUADRANT) + q), QUADRANT * q + SCALE_ROWS * a)
            for a in range(PASSES)
            for q in range(P // QUADRANT)
        ]
        for i, (source, target) in enumerate(moves[1:]):
            queue = nc.scalar if i < 3 else nc.sync
            queue.dma_start(
                out=planes[target : target + SCALE_ROWS, :].bitcast(I32),
                in_=picked_bytes[source : source + SCALE_ROWS, :].bitcast(I32),
            )
        words0 = keep.tile([P, S], U32, name="words0", align_bytes=64)
        nc.vector.tensor_copy(words0[:], word_window[0][:].indirect(offsets[:]))

        w_grouped = keep.tile([P, PASSES, N, PACK], BF16, name="w_grouped", align_bytes=64)
        w_codes = keep.tile([P, PASSES, N], U32, name="w_codes", align_bytes=64)
        w_scales = keep.tile([P, PASSES, N], U8, name="w_scales", align_bytes=64)
        nc.scalar.activation(w_grouped[:], w_raw[:].rearrange("p a j n -> p a n j"), ACT.Copy)
        nc.vector.quantize_mx(
            out=w_codes[:].rearrange("p a n -> p (a n)").bitcast(FP8X4),
            scales=w_scales[:].rearrange("p a n -> p (a n)"),
            in_=w_grouped[:].rearrange("p a n j -> p (a n j)"),
        )

        weights = keep.tile([P, S], F32, name="weights", tag="w_then_wt")
        nc.sync.dma_start(out=weights[:], in_=wt)

        def chunk_steps(c, j0, n):
            nv = n // D
            nw = nv // D

            def sb(name, shape):
                return keep.tile([P] + shape, F32, name="%s%d" % (name, c))

            y = psum.tile([P, n], F32, name="y%d" % c)
            upper = sb("upper", [2, nv])
            pair_sum = sb("pair_sum", [2, nv])
            pair_diff = sb("pair_diff", [2, nv])
            pair_sq = sb("pair_sq", [2, nv])
            sum4 = sb("sum4", [nv])
            cross = sb("cross", [nv])
            cross_sq = sb("cross_sq", [nv])
            within = sb("within", [nv])
            within_all = sb("within_all", [nv])
            sum16 = sb("sum16", [nw])
            gap4 = sb("gap4", [nv])
            gap_sq = sb("gap_sq", [nv])
            between = sb("between", [nw])
            den = sb("den", [nv])
            root = sb("root", [nv])
            inv = sb("inv", [nv])
            shr = sb("shr", [nv])
            scaled_gap4 = sb("scaled_gap4", [nv])
            pull4 = sb("pull4", [nv])
            post4 = sb("post4", [nv])
            resid = sb("resid", [n])
            resid_sq = sb("resid_sq", [n])
            weighted = sb("weighted", [n])
            result = sb("result", [n])
            members = y[:].rearrange("p (v d) -> p d v", d=D)

            def product():
                words1 = keep.tile([P, n], U32, name="words1_%d" % c, align_bytes=64)
                first = j0 // LIST_COLUMN
                nc.vector.tensor_copy(
                    words1[:], word_window[1][:].indirect(offsets[:, first : first + n // LIST_COLUMN])
                )
                for i0 in range(0, n, PIECE):
                    m = min(PIECE, n - i0)
                    for a, moving in enumerate((words0[:, j0 + i0 : j0 + i0 + m], words1[:, i0 : i0 + m])):
                        nc.tensor.matmul_mx(
                            out=y[:, i0 : i0 + m],
                            lhsT=w_codes[:, a, :].bitcast(FP8X4),
                            lhsT_scale=w_scales[:, a, :],
                            rhs=moving.bitcast(FP8X4),
                            rhs_scale=planes[SCALE_ROWS * a : P, j0 + i0 : j0 + i0 + m],
                            start=(a == 0),
                            stop=(a == PASSES - 1),
                        )
                nc.scalar.copy(upper[:], members[:, 2:4, :])

            def pairs():
                nc.vector.tensor_tensor(pair_sum[:], members[:, 0:2, :], upper[:], ALU.add)
                nc.vector.tensor_tensor(pair_diff[:], members[:, 0:2, :], upper[:], ALU.subtract)
                nc.scalar.activation(pair_sq[:], pair_diff[:], ACT.Square, scale=math.sqrt(1.0 / 32.0))

            def district_sums():
                nc.vector.tensor_tensor(sum4[:], pair_sum[:, 0, :], pair_sum[:, 1, :], ALU.add)
                nc.vector.tensor_tensor(cross[:], pair_sum[:, 0, :], pair_sum[:, 1, :], ALU.subtract)
                nc.scalar.activation(cross_sq[:], cross[:], ACT.Square, scale=0.125)

            def state_sums():
                nc.vector.tensor_reduce(sum16[:], by_group(sum4[:]), AXIS.X, ALU.add)

            def gaps():
                nc.vector.scalar_tensor_tensor(
                    by_group(gap4[:]), over_members(sum16[:], nw), -0.25, by_group(sum4[:]), ALU.mult, ALU.add
                )
                nc.scalar.activation(gap_sq[:], gap4[:], ACT.Square, scale=0.125)
                nc.vector.tensor_tensor(within[:], pair_sq[:, 0, :], pair_sq[:, 1, :], ALU.add)

            def within_variance():
                nc.vector.scalar_tensor_tensor(within_all[:], within[:], 0.075, cross_sq[:], ALU.add, ALU.add)

            def between_variance():
                nc.vector.tensor_reduce(between[:], by_group(gap_sq[:]), AXIS.X, ALU.add)

            def denominator():
                nc.vector.tensor_tensor(by_group(den[:]), by_group(within_all[:]), over_members(between[:], nw), ALU.add)
                nc.scalar.activation(root[:], den[:], ACT.Abs_reciprocal_sqrt)
                nc.scalar.activation(inv[:], root[:], ACT.Square)

            def numerator():
                nc.vector.scalar_tensor_tensor(
                    by_group(scaled_gap4[:]), over_members(between[:], nw), 0.05, by_group(gap4[:]), ALU.add, ALU.mult
                )

            def pull():
                nc.vector.tensor_tensor(pull4[:], scaled_gap4[:], inv[:], ALU.mult)

            def posterior():
                nc.vector.scalar_tensor_tensor(
                    by_group(post4[:]), over_members(sum16[:], nw), 0.25, by_group(pull4[:]), ALU.mult, ALU.add
                )
                nc.vector.scalar_tensor_tensor(
                    by_group(shr[:]), over_members(between[:], nw), 0.05, by_group(inv[:]), ALU.add, ALU.mult
                )

            width = 128 if c == len(CHUNKS) - 1 else FINAL
            parts = [(i0, min(width, n - i0)) for i0 in range(0, n, width)]

            def residual():
                for i0, m in parts:
                    js, vs = slice(i0, i0 + m), slice(i0 // D, (i0 + m) // D)
                    nc.vector.scalar_tensor_tensor(
                        by_group(resid[:, js]), over_members(post4[:, vs], m // D), -0.25, by_group(y[:, js]),
                        ALU.mult, ALU.add,
                    )
                    nc.scalar.activation(resid_sq[:, js], resid[:, js], ACT.Square)

            def weigh():
                for i0, m in parts:
                    js = slice(i0, i0 + m)
                    nc.vector.tensor_tensor(weighted[:, js], resid_sq[:, js], weights[:, j0 + i0 : j0 + i0 + m], ALU.mult)

            def finish():
                for i0, m in parts:
                    js, vs = slice(i0, i0 + m), slice(i0 // D, (i0 + m) // D)
                    nc.vector.tensor_tensor(
                        by_group(result[:, js]), by_group(weighted[:, js]), over_members(shr[:, vs], m // D), ALU.add
                    )
                    nc.sync.dma_start(out=out[:, j0 + i0 : j0 + i0 + m], in_=result[:, js])

            return [product, pairs, district_sums, state_sums, gaps, within_variance, between_variance,
                    denominator, numerator, pull, posterior, residual, weigh, finish]

        starts = [sum(CHUNKS[:c]) for c in range(len(CHUNKS))]
        steps = [chunk_steps(c, starts[c], CHUNKS[c]) for c in range(len(CHUNKS))]
        depth = len(steps[0])
        for tick in range(depth + SKEW * (len(CHUNKS) - 1)):
            for c in range(len(CHUNKS)):
                k = tick - SKEW * c
                if 0 <= k < depth:
                    steps[c][k]()
